import numpy as np
import ml_dtypes


def mxq(x, axis, fmt="e4m3"):
    dtype, down = {"e4m3": (ml_dtypes.float8_e4m3fn, 7), "e5m2": (ml_dtypes.float8_e5m2, 14)}[fmt]
    v = np.moveaxis(np.asarray(x, np.float32).astype(ml_dtypes.bfloat16).astype(np.float64), axis, -1)
    blocks = v.reshape(v.shape[:-1] + (-1, 32))
    amax = np.abs(blocks).max(-1, keepdims=True)
    byte = np.maximum(np.where(amax > 0, np.frexp(amax)[1] - 1 + 127, 0) - down, 1)
    scale = np.exp2(byte - 127.0)
    codes = (blocks / scale).astype(np.float32).astype(dtype).astype(np.float64)
    return np.moveaxis((codes * scale).reshape(v.shape), -1, axis)


WIDE = False


def mx_kscale(k):
    if not WIDE:
        return np.ones(k)
    levels = np.array([30, -30])
    if k % 512:
        return np.exp2(np.random.permutation(np.resize(levels, k // 32))).repeat(32)
    a = np.empty((k // 512, 16))
    for p in range(k // 512):
        a[p, :8] = np.random.permutation(np.resize(levels, 8))
        for g in range(8):
            far = levels[np.abs(levels - a[p, g]) >= 10]
            a[p, g + 8] = far[np.random.randint(len(far))]
    return np.exp2(a.ravel()).repeat(32)


def f64(x):
    return np.asarray(x).astype(np.float64)


def striped(idx):
    return np.tile(np.asarray(idx).reshape(-1, 16).T, (8, 1)).astype(np.uint16)


def unstriped(offs):
    return offs[:16].T.reshape(-1).astype(np.int64)


E2M1 = np.array([0.0, 0.5, 1.0, 1.5, 2.0, 3.0, 4.0, 6.0, -0.0, -0.5, -1.0, -1.5, -2.0, -3.0, -4.0, -6.0])


def pack_weight(w, fmt):
    k, n = w.shape
    w = f64(np.asarray(w, np.float32).astype(ml_dtypes.bfloat16)).reshape(k // 32, 32, n)
    amax = np.abs(w).max(1)
    if fmt in ("e4m3", "e5m2"):
        byte = np.frexp(amax)[1] - 1 + 127 - (7 if fmt == "e4m3" else 14)
    else:
        mant, ex = np.frexp(amax / 6.0)
        byte = np.where(mant > 0.5, ex, ex - 1) + 127
    byte = np.clip(np.where(amax > 0, byte, 1), 1, 254)
    scaled = (w * np.exp2(127.0 - byte)[:, None, :]).reshape(k, n).astype(np.float32)
    by_word = np.ascontiguousarray(scaled.reshape(k // 512, 128, 4, n).transpose(0, 1, 3, 2))
    if fmt in ("e4m3", "e5m2"):
        words = by_word.astype(ml_dtypes.float8_e4m3fn if fmt == "e4m3" else ml_dtypes.float8_e5m2).view(np.uint8)
    else:
        c = by_word.astype(ml_dtypes.float4_e2m1fn).view(np.uint8) & 0xF
        words = (c[..., 0::2] | (c[..., 1::2] << 4)).reshape(k // 512, 128, 2 * n)
    return np.ascontiguousarray(words), np.ascontiguousarray(byte.astype(np.uint8).reshape(k // 512, 16, n))


def unpack_weight(words, scales, fmt):
    g, _, n = scales.shape
    words = np.ascontiguousarray(words).reshape(g, 128, n, -1)
    if fmt in ("e4m3", "e5m2"):
        vals = words.view(ml_dtypes.float8_e4m3fn if fmt == "e4m3" else ml_dtypes.float8_e5m2).astype(np.float64)
    else:
        nib = np.empty((g, 128, n, 4), np.uint8)
        nib[..., 0::2] = words & 0xF
        nib[..., 1::2] = words >> 4
        vals = E2M1[nib]
    vals = vals * np.repeat(np.exp2(scales.astype(np.float64) - 127.0), 8, axis=1)[..., None]
    return vals.transpose(0, 1, 3, 2).reshape(g * 512, n)


K, T, J, N, L = 1024, 1024, 256, 256, 512


def setup_inputs():
    n = np.random.standard_normal
    idx = np.random.permutation(T)[:J]
    fk = mx_kscale(K)
    fl = mx_kscale(L)
    xtp = pack_weight(n((K, T)) * np.random.uniform(0.4, 1.6, (1, T)) / fk[:, None], "e2m1")
    wap = pack_weight(n((K, N)) * 1 / np.sqrt(K) * fk[:, None], "e5m2")
    wbp = pack_weight(n((L, N)) * 1 / np.sqrt(L) * fl[:, None], "e4m3")
    return {
        "xt_words": xtp[0],
        "xt_scales": xtp[1],
        "wa_words": wap[0],
        "wa_scales": wap[1],
        "sx": (n((L, J)) * np.random.uniform(0.4, 1.6, (1, J)) / fl[:, None]).astype(np.float32),
        "wb_words": wbp[0],
        "wb_scales": wbp[1],
        "bi": (np.random.uniform(-0.6, 0.6, (1, N))).astype(np.float32),
        "offs": striped(idx),
    }


def reference(xt_words, xt_scales, wa_words, wa_scales, sx, wb_words, wb_scales, bi, offs):
    idx = unstriped(offs)
    xtu = unpack_weight(xt_words, xt_scales, "e2m1")
    wau = unpack_weight(wa_words, wa_scales, "e5m2")
    wbu = unpack_weight(wb_words, wb_scales, "e4m3")
    xtidxg = xtu[:, idx]
    a = xtidxg.T @ wau
    sxq = mxq(f64(sx), 0, "e5m2")
    b0 = sxq.T @ wbu
    b2 = b0 + f64(bi)
    e = np.exp(0.6 * (a - b2))
    y = 256.0 * e / np.sum(e, axis=1, keepdims=True)
    return y

@@ -1,0 +1,180 @@
+from contextlib import ExitStack
+
+import concourse.mybir as mybir
+from concourse.masks import make_identity
+
+K, T, J, N, L = 1024, 1024, 256, 256, 512
+FLOPS = 2 * J * N * (K + L)
+
+F32 = mybir.dt.float32
+BF16 = mybir.dt.bfloat16
+I32 = mybir.dt.int32
+U32 = mybir.dt.uint32
+U16 = mybir.dt.uint16
+U8 = mybir.dt.uint8
+E2M1 = mybir.dt.float4_e2m1fn_x4
+E5M2 = mybir.dt.float8_e5m2_x4
+E4M3 = mybir.dt.float8_e4m3fn_x4
+ALU = mybir.AluOpType
+ACT = mybir.ActivationFunctionType
+
+P = 128
+PACK = 4
+PASSES = K // (P * PACK)
+TILES = J // P
+QUADRANTS = 4
+SHARPNESS = 0.6
+
+
+def tile_list_rows_owninput_sharesofgap_kernel(
+    tc, xt_words, xt_scales, wa_words, wa_scales, sx, wb_words, wb_scales, bi, offs, out
+):
+    nc = tc.nc
+    with ExitStack() as ctx:
+        sb = ctx.enter_context(tc.tile_pool(name="sb", bufs=1))
+        ps = ctx.enter_context(tc.psum_pool(name="ps", bufs=1))
+
+        offsets = sb.tile([P, J // 16], U16, name="offsets")
+        xt_table = [sb.tile([P, T], U16, name=f"xt_table{z}", align_bytes=64) for z in range(PASSES)]
+        xt_planes = sb.tile([P, PASSES * T], U8, name="xt_planes", align_bytes=64)
+        wa_planes = sb.tile([P, PASSES * N], U8, name="wa_planes", align_bytes=64)
+        wb_plane = sb.tile([P, N], U8, name="wb_plane", align_bytes=64)
+        wa_codes = sb.tile([P, PASSES * N], U32, name="wa_codes", align_bytes=64)
+        wb_codes = sb.tile([P, N], U32, name="wb_codes", align_bytes=64)
+        sx_rows = sb.tile([P, PACK, J], F32, name="sx_rows", align_bytes=64)
+        bias_pairs = sb.tile([P, 2], F32, name="bias_pairs")
+        identity = sb.tile([P, P], F32, name="identity")
+
+        nc.vector.memset(xt_planes[:].bitcast(I32), 0)
+        nc.vector.memset(wb_plane[:].bitcast(I32), 0)
+        nc.vector.memset(wa_planes[:].bitcast(I32), 0)
+
+        def load_scale_rows(queue, planes, scales, q):
+            queue.dma_start(
+                out=planes[32 * q : 32 * q + 4, :].bitcast(I32).rearrange("r (z c) -> r z c", z=scales.shape[0]),
+                in_=scales[:, 4 * q : 4 * q + 4, :].bitcast(I32).rearrange("z r c -> r z c"),
+            )
+
+        def load_table(z):
+            nc.sync.dma_start(out=xt_table[z][:].bitcast(I32), in_=xt_words[z].bitcast(I32))
+
+        def load_sx():
+            nc.sync.dma_start(out=sx_rows[:], in_=sx.rearrange("(p t) j -> p t j", t=PACK))
+
+        def load_wa():
+            nc.sync.dma_start(
+                out=wa_codes[:].bitcast(I32).rearrange("p (z n) -> p z n", z=PASSES),
+                in_=wa_words.rearrange("z p n t -> p z (n t)").bitcast(I32),
+            )
+
+        def load_wb():
+            nc.sync.dma_start(out=wb_codes[:].bitcast(I32), in_=wb_words[0].rearrange("p n t -> p (n t)").bitcast(I32))
+
+        def load_bias(queue):
+            queue.dma_start(out=bias_pairs[:], in_=bi.rearrange("o (p c) -> p (o c)", c=2))
+
+        nc.sync.dma_start(offsets[:], offs)
+        load_table(0)
+        for q in range(QUADRANTS):
+            load_scale_rows(nc.sync, xt_planes, xt_scales, q)
+        load_bias(nc.sync)
+        load_sx()
+        load_scale_rows(nc.sync, wa_planes, wa_scales, 0)
+        load_wa()
+        for q in range(1, QUADRANTS):
+            load_scale_rows(nc.sync, wa_planes, wa_scales, q)
+        load_wb()
+        load_table(1)
+        for q in range(2):
+            load_scale_rows(nc.sync, wb_plane, wb_scales, q)
+        for q in range(2, QUADRANTS):
+            load_scale_rows(nc.gpsimd, wb_plane, wb_scales, q)
+        make_identity(nc, identity[:])
+
+        bias_bank = ps.tile([P, 2, P], F32, name="bias_bank")
+        for c in range(2):
+            nc.tensor.transpose(bias_bank[:, c, :], bias_pairs[:, c : c + 1].to_broadcast([P, P]), identity[:])
+        bias_rows = sb.tile([P, N], F32, name="bias_rows")
+
+        picked_words = [sb.tile([P, J], U16, name=f"picked_words{z}", align_bytes=64) for z in range(PASSES)]
+        picked_planes = [sb.tile([P, J], U8, name=f"picked_plane{z}", align_bytes=64) for z in range(PASSES)]
+        nc.vector.tensor_copy(picked_words[0][:], xt_table[0][:].indirect(offsets[:]))
+        for z in range(PASSES):
+            nc.vector.tensor_copy(picked_planes[z][:], xt_planes[:, z * T : (z + 1) * T].indirect(offsets[:]))
+
+        sx_grouped = sb.tile([P, J * PACK], BF16, name="sx_grouped", align_bytes=64)
+        sx_codes = sb.tile([P, J], U32, name="sx_codes", align_bytes=64)
+        sx_plane = sb.tile([P, J], U8, name="sx_plane", align_bytes=64)
+        for h in range(TILES):
+            cols = slice(h * P, (h + 1) * P)
+            grouped = sx_grouped[:, h * P * PACK : (h + 1) * P * PACK]
+            nc.scalar.activation(
+                out=grouped.rearrange("p (c i t) -> p c t i", i=4, t=PACK),
+                in_=sx_rows[:, :, cols].rearrange("p t (c i) -> p c t i", i=4),
+                func=ACT.Copy,
+                scale=-1.0,
+            )
+            nc.vector.quantize_mx(out=sx_codes[:, cols].bitcast(E5M2), scales=sx_plane[:, cols], in_=grouped)
+
+        nc.scalar.activation(
+            out=bias_rows[:].rearrange("p (i c) -> p i c", c=2),
+            in_=bias_bank[:].rearrange("p c i -> p i c"),
+            func=ACT.Copy,
+            scale=SHARPNESS,
+        )
+
+        for h in range(TILES):
+            nc.vector.tensor_copy(
+                picked_words[1][:, h * P : (h + 1) * P], xt_table[1][:].indirect(offsets[:, h * 8 : (h + 1) * 8])
+            )
+
+        gap = [ps.tile([P, N], F32, name=f"gap{h}") for h in range(TILES)]
+
+        def token_pass(h, z, start, stop):
+            cols = slice(h * P, (h + 1) * P)
+            nc.tensor.matmul_mx(
+                out=gap[h][:],
+                lhsT=picked_words[z][:, cols].bitcast(E2M1),
+                lhsT_scale=picked_planes[z][:, cols],
+                rhs=wa_codes[:, z * N : (z + 1) * N].bitcast(E5M2),
+                rhs_scale=wa_planes[:, z * N : (z + 1) * N],
+                start=start,
+                stop=stop,
+            )
+
+        for h in range(TILES):
+            token_pass(h, 0, True, False)
+        for h in range(TILES):
+            cols = slice(h * P, (h + 1) * P)
+            nc.tensor.matmul_mx(
+                out=gap[h][:],
+                lhsT=sx_codes[:, cols].bitcast(E5M2),
+                lhsT_scale=sx_plane[:, cols],
+                rhs=wb_codes[:].bitcast(E4M3),
+                rhs_scale=wb_plane[:],
+                start=False,
+                stop=False,
+            )
+        for h in range(TILES):
+            token_pass(h, 1, False, True)
+
+        negated = [sb.tile([P, N], F32, name=f"negated{h}") for h in range(TILES)]
+        least = [sb.tile([P, 1], F32, name=f"least{h}") for h in range(TILES)]
+        total = [sb.tile([P, 1], F32, name=f"total{h}") for h in range(TILES)]
+        inverse = [sb.tile([P, 1], F32, name=f"inverse{h}") for h in range(TILES)]
+        powers = [sb.tile([P, N], F32, name=f"powers{h}") for h in range(TILES)]
+        shares = [sb.tile([P, N], F32, name=f"shares{h}") for h in range(TILES)]
+        for h in range(TILES):
+            nc.vector.scalar_tensor_tensor(
+                out=negated[h][:], in0=gap[h][:], scalar=-SHARPNESS, in1=bias_rows[:], op0=ALU.mult, op1=ALU.add
+            )
+            nc.vector.tensor_reduce(out=least[h][:], in_=negated[h][:], axis=mybir.AxisListType.X, op=ALU.min)
+            nc.scalar.activation(
+                out=powers[h][:], in_=negated[h][:], func=ACT.Exp, bias=least[h][:], scale=-1.0, accum_out=total[h][:]
+            )
+        for h in range(TILES):
+            nc.vector.reciprocal(out=inverse[h][:], in_=total[h][:])
+            nc.vector.tensor_scalar(
+                out=shares[h][:], in0=powers[h][:], scalar1=inverse[h][:], scalar2=float(N), op0=ALU.mult, op1=ALU.mult
+            )
+            nc.sync.dma_start(out=out[h * P : (h + 1) * P, :], in_=shares[h][:])

@@ -45,9 +45,11 @@ def tile_list_rows_owninput_sharesofgap_kernel(
         bias_pairs = sb.tile([P, 2], F32, name="bias_pairs")
         identity = sb.tile([P, P], F32, name="identity")
 
-        nc.vector.memset(xt_planes[:].bitcast(I32), 0)
-        nc.vector.memset(wb_plane[:].bitcast(I32), 0)
+        nc.vector.memset(xt_planes[:, :T].bitcast(I32), 0)
+        nc.gpsimd.memset(xt_planes[:, T:].bitcast(I32), 0)
         nc.vector.memset(wa_planes[:].bitcast(I32), 0)
+        nc.vector.memset(wb_plane[:].bitcast(I32), 0)
+        nc.vector.memset(identity[:], 0.0)
 
         def load_scale_rows(queue, planes, scales, q):
             queue.dma_start(
@@ -73,23 +75,23 @@ def tile_list_rows_owninput_sharesofgap_kernel(
         def load_bias(queue):
             queue.dma_start(out=bias_pairs[:], in_=bi.rearrange("o (p c) -> p (o c)", c=2))
 
-        nc.sync.dma_start(offsets[:], offs)
         load_table(0)
+        nc.sync.dma_start(offsets[:], offs)
+        load_wa()
         for q in range(QUADRANTS):
             load_scale_rows(nc.sync, xt_planes, xt_scales, q)
-        load_bias(nc.sync)
         load_sx()
-        load_scale_rows(nc.sync, wa_planes, wa_scales, 0)
-        load_wa()
-        for q in range(1, QUADRANTS):
+        for q in range(2):
             load_scale_rows(nc.sync, wa_planes, wa_scales, q)
         load_wb()
         load_table(1)
-        for q in range(2):
+        for q in range(3):
             load_scale_rows(nc.sync, wb_plane, wb_scales, q)
+        load_bias(nc.gpsimd)
         for q in range(2, QUADRANTS):
-            load_scale_rows(nc.gpsimd, wb_plane, wb_scales, q)
-        make_identity(nc, identity[:])
+            load_scale_rows(nc.gpsimd, wa_planes, wa_scales, q)
+        make_identity(nc, identity[:], nomemset=True)
+        load_scale_rows(nc.gpsimd, wb_plane, wb_scales, 3)
 
         bias_bank = ps.tile([P, 2, P], F32, name="bias_bank")
         for c in range(2):

@@ -47,9 +47,9 @@ def tile_list_rows_owninput_sharesofgap_kernel(
 
         nc.vector.memset(xt_planes[:, :T].bitcast(I32), 0)
         nc.gpsimd.memset(xt_planes[:, T:].bitcast(I32), 0)
+        nc.vector.memset(identity[:], 0.0)
         nc.vector.memset(wa_planes[:].bitcast(I32), 0)
         nc.vector.memset(wb_plane[:].bitcast(I32), 0)
-        nc.vector.memset(identity[:], 0.0)
 
         def load_scale_rows(queue, planes, scales, q):
             queue.dma_start(
@@ -75,23 +75,22 @@ def tile_list_rows_owninput_sharesofgap_kernel(
         def load_bias(queue):
             queue.dma_start(out=bias_pairs[:], in_=bi.rearrange("o (p c) -> p (o c)", c=2))
 
-        load_table(0)
         nc.sync.dma_start(offsets[:], offs)
-        load_wa()
+        load_table(0)
+        load_bias(nc.sync)
         for q in range(QUADRANTS):
             load_scale_rows(nc.sync, xt_planes, xt_scales, q)
         load_sx()
+        load_table(1)
         for q in range(2):
             load_scale_rows(nc.sync, wa_planes, wa_scales, q)
-        load_wb()
-        load_table(1)
-        for q in range(3):
-            load_scale_rows(nc.sync, wb_plane, wb_scales, q)
-        load_bias(nc.gpsimd)
+        load_wa()
         for q in range(2, QUADRANTS):
-            load_scale_rows(nc.gpsimd, wa_planes, wa_scales, q)
+            load_scale_rows(nc.sync, wa_planes, wa_scales, q)
+        load_wb()
+        for q in range(QUADRANTS):
+            load_scale_rows(nc.sync, wb_plane, wb_scales, q)
         make_identity(nc, identity[:], nomemset=True)
-        load_scale_rows(nc.gpsimd, wb_plane, wb_scales, 3)
 
         bias_bank = ps.tile([P, 2, P], F32, name="bias_bank")
         for c in range(2):
@@ -111,8 +110,8 @@ def tile_list_rows_owninput_sharesofgap_kernel(
             cols = slice(h * P, (h + 1) * P)
             grouped = sx_grouped[:, h * P * PACK : (h + 1) * P * PACK]
             nc.scalar.activation(
-                out=grouped.rearrange("p (c i t) -> p c t i", i=4, t=PACK),
-                in_=sx_rows[:, :, cols].rearrange("p t (c i) -> p c t i", i=4),
+                out=grouped.rearrange("p (c t) -> p c t", t=PACK),
+                in_=sx_rows[:, :, cols].rearrange("p t c -> p c t"),
                 func=ACT.Copy,
                 scale=-1.0,
             )
@@ -145,9 +144,9 @@ def tile_list_rows_owninput_sharesofgap_kernel(
             )
 
         for h in range(TILES):
-            token_pass(h, 0, True, False)
-        for h in range(TILES):
             cols = slice(h * P, (h + 1) * P)
+            token_pass(h, 0, True, False)
+            token_pass(h, 1, False, False)
             nc.tensor.matmul_mx(
                 out=gap[h][:],
                 lhsT=sx_codes[:, cols].bitcast(E5M2),
@@ -155,10 +154,8 @@ def tile_list_rows_owninput_sharesofgap_kernel(
                 rhs=wb_codes[:].bitcast(E4M3),
                 rhs_scale=wb_plane[:],
                 start=False,
-                stop=False,
+                stop=True,
             )
-        for h in range(TILES):
-            token_pass(h, 1, False, True)
 
         negated = [sb.tile([P, N], F32, name=f"negated{h}") for h in range(TILES)]
         least = [sb.tile([P, 1], F32, name=f"least{h}") for h in range(TILES)]

from contextlib import ExitStack

import concourse.mybir as mybir
from concourse.masks import make_identity

K, T, J, N, L = 1024, 1024, 256, 256, 512
FLOPS = 2 * J * N * (K + L)

F32 = mybir.dt.float32
BF16 = mybir.dt.bfloat16
I32 = mybir.dt.int32
U32 = mybir.dt.uint32
U16 = mybir.dt.uint16
U8 = mybir.dt.uint8
E2M1 = mybir.dt.float4_e2m1fn_x4
E5M2 = mybir.dt.float8_e5m2_x4
E4M3 = mybir.dt.float8_e4m3fn_x4
ALU = mybir.AluOpType
ACT = mybir.ActivationFunctionType

P = 128
PACK = 4
PASSES = K // (P * PACK)
TILES = J // P
QUADRANTS = 4
SHARPNESS = 0.6


def tile_list_rows_owninput_sharesofgap_kernel(
    tc, xt_words, xt_scales, wa_words, wa_scales, sx, wb_words, wb_scales, bi, offs, out
):
    nc = tc.nc
    with ExitStack() as ctx:
        sb = ctx.enter_context(tc.tile_pool(name="sb", bufs=1))
        ps = ctx.enter_context(tc.psum_pool(name="ps", bufs=1))

        offsets = sb.tile([P, J // 16], U16, name="offsets")
        xt_table = [sb.tile([P, T], U16, name=f"xt_table{z}", align_bytes=64) for z in range(PASSES)]
        xt_planes = sb.tile([P, PASSES * T], U8, name="xt_planes", align_bytes=64)
        wa_planes = sb.tile([P, PASSES * N], U8, name="wa_planes", align_bytes=64)
        wb_plane = sb.tile([P, N], U8, name="wb_plane", align_bytes=64)
        wa_codes = sb.tile([P, PASSES * N], U32, name="wa_codes", align_bytes=64)
        wb_codes = sb.tile([P, N], U32, name="wb_codes", align_bytes=64)
        sx_rows = sb.tile([P, PACK, J], F32, name="sx_rows", align_bytes=64)
        bias_pairs = sb.tile([P, 2], F32, name="bias_pairs")
        identity = sb.tile([P, P], F32, name="identity")

        nc.vector.memset(xt_planes[:, :T].bitcast(I32), 0)
        nc.gpsimd.memset(xt_planes[:, T:].bitcast(I32), 0)
        nc.vector.memset(identity[:], 0.0)
        nc.vector.memset(wa_planes[:].bitcast(I32), 0)
        nc.vector.memset(wb_plane[:].bitcast(I32), 0)

        def load_scale_rows(queue, planes, scales, q):
            queue.dma_start(
                out=planes[32 * q : 32 * q + 4, :].bitcast(I32).rearrange("r (z c) -> r z c", z=scales.shape[0]),
                in_=scales[:, 4 * q : 4 * q + 4, :].bitcast(I32).rearrange("z r c -> r z c"),
            )

        def load_table(z):
            nc.sync.dma_start(out=xt_table[z][:].bitcast(I32), in_=xt_words[z].bitcast(I32))

        def load_sx():
            nc.sync.dma_start(out=sx_rows[:], in_=sx.rearrange("(p t) j -> p t j", t=PACK))

        def load_wa():
            nc.sync.dma_start(
                out=wa_codes[:].bitcast(I32).rearrange("p (z n) -> p z n", z=PASSES),
                in_=wa_words.rearrange("z p n t -> p z (n t)").bitcast(I32),
            )

        def load_wb():
            nc.sync.dma_start(out=wb_codes[:].bitcast(I32), in_=wb_words[0].rearrange("p n t -> p (n t)").bitcast(I32))

        def load_bias(queue):
            queue.dma_start(out=bias_pairs[:], in_=bi.rearrange("o (p c) -> p (o c)", c=2))

        nc.sync.dma_start(offsets[:], offs)
        load_table(0)
        load_bias(nc.sync)
        for q in range(QUADRANTS):
            load_scale_rows(nc.sync, xt_planes, xt_scales, q)
        load_sx()
        load_table(1)
        for q in range(2):
            load_scale_rows(nc.sync, wa_planes, wa_scales, q)
        load_wa()
        for q in range(2, QUADRANTS):
            load_scale_rows(nc.sync, wa_planes, wa_scales, q)
        load_wb()
        for q in range(QUADRANTS):
            load_scale_rows(nc.sync, wb_plane, wb_scales, q)
        make_identity(nc, identity[:], nomemset=True)

        bias_bank = ps.tile([P, 2, P], F32, name="bias_bank")
        for c in range(2):
            nc.tensor.transpose(bias_bank[:, c, :], bias_pairs[:, c : c + 1].to_broadcast([P, P]), identity[:])
        bias_rows = sb.tile([P, N], F32, name="bias_rows")

        picked_words = [sb.tile([P, J], U16, name=f"picked_words{z}", align_bytes=64) for z in range(PASSES)]
        picked_planes = [sb.tile([P, J], U8, name=f"picked_plane{z}", align_bytes=64) for z in range(PASSES)]
        nc.vector.tensor_copy(picked_words[0][:], xt_table[0][:].indirect(offsets[:]))
        for z in range(PASSES):
            nc.vector.tensor_copy(picked_planes[z][:], xt_planes[:, z * T : (z + 1) * T].indirect(offsets[:]))

        sx_grouped = sb.tile([P, J * PACK], BF16, name="sx_grouped", align_bytes=64)
        sx_codes = sb.tile([P, J], U32, name="sx_codes", align_bytes=64)
        sx_plane = sb.tile([P, J], U8, name="sx_plane", align_bytes=64)
        for h in range(TILES):
            cols = slice(h * P, (h + 1) * P)
            grouped = sx_grouped[:, h * P * PACK : (h + 1) * P * PACK]
            nc.scalar.activation(
                out=grouped.rearrange("p (c t) -> p c t", t=PACK),
                in_=sx_rows[:, :, cols].rearrange("p t c -> p c t"),
                func=ACT.Copy,
                scale=-1.0,
            )
            nc.vector.quantize_mx(out=sx_codes[:, cols].bitcast(E5M2), scales=sx_plane[:, cols], in_=grouped)

        nc.scalar.activation(
            out=bias_rows[:].rearrange("p (i c) -> p i c", c=2),
            in_=bias_bank[:].rearrange("p c i -> p i c"),
            func=ACT.Copy,
            scale=SHARPNESS,
        )

        for h in range(TILES):
            nc.vector.tensor_copy(
                picked_words[1][:, h * P : (h + 1) * P], xt_table[1][:].indirect(offsets[:, h * 8 : (h + 1) * 8])
            )

        gap = [ps.tile([P, N], F32, name=f"gap{h}") for h in range(TILES)]

        def token_pass(h, z, start, stop):
            cols = slice(h * P, (h + 1) * P)
            nc.tensor.matmul_mx(
                out=gap[h][:],
                lhsT=picked_words[z][:, cols].bitcast(E2M1),
                lhsT_scale=picked_planes[z][:, cols],
                rhs=wa_codes[:, z * N : (z + 1) * N].bitcast(E5M2),
                rhs_scale=wa_planes[:, z * N : (z + 1) * N],
                start=start,
                stop=stop,
            )

        for h in range(TILES):
            cols = slice(h * P, (h + 1) * P)
            token_pass(h, 0, True, False)
            token_pass(h, 1, False, False)
            nc.tensor.matmul_mx(
                out=gap[h][:],
                lhsT=sx_codes[:, cols].bitcast(E5M2),
                lhsT_scale=sx_plane[:, cols],
                rhs=wb_codes[:].bitcast(E4M3),
                rhs_scale=wb_plane[:],
                start=False,
                stop=True,
            )

        negated = [sb.tile([P, N], F32, name=f"negated{h}") for h in range(TILES)]
        least = [sb.tile([P, 1], F32, name=f"least{h}") for h in range(TILES)]
        total = [sb.tile([P, 1], F32, name=f"total{h}") for h in range(TILES)]
        inverse = [sb.tile([P, 1], F32, name=f"inverse{h}") for h in range(TILES)]
        powers = [sb.tile([P, N], F32, name=f"powers{h}") for h in range(TILES)]
        shares = [sb.tile([P, N], F32, name=f"shares{h}") for h in range(TILES)]
        for h in range(TILES):
            nc.vector.scalar_tensor_tensor(
                out=negated[h][:], in0=gap[h][:], scalar=-SHARPNESS, in1=bias_rows[:], op0=ALU.mult, op1=ALU.add
            )
            nc.vector.tensor_reduce(out=least[h][:], in_=negated[h][:], axis=mybir.AxisListType.X, op=ALU.min)
            nc.scalar.activation(
                out=powers[h][:], in_=negated[h][:], func=ACT.Exp, bias=least[h][:], scale=-1.0, accum_out=total[h][:]
            )
        for h in range(TILES):
            nc.vector.reciprocal(out=inverse[h][:], in_=total[h][:])
            nc.vector.tensor_scalar(
                out=shares[h][:], in0=powers[h][:], scalar1=inverse[h][:], scalar2=float(N), op0=ALU.mult, op1=ALU.mult
            )
            nc.sync.dma_start(out=out[h * P : (h + 1) * P, :], in_=shares[h][:])
